import numpy as np
import ml_dtypes


def mxq(x, axis, fmt="e4m3"):
    dtype, down = {"e4m3": (ml_dtypes.float8_e4m3fn, 7), "e5m2": (ml_dtypes.float8_e5m2, 14)}[fmt]
    v = np.moveaxis(np.asarray(x, np.float32).astype(ml_dtypes.bfloat16).astype(np.float64), axis, -1)
    blocks = v.reshape(v.shape[:-1] + (-1, 32))
    amax = np.abs(blocks).max(-1, keepdims=True)
    byte = np.maximum(np.where(amax > 0, np.frexp(amax)[1] - 1 + 127, 0) - down, 1)
    scale = np.exp2(byte - 127.0)
    codes = (blocks / scale).astype(np.float32).astype(dtype).astype(np.float64)
    return np.moveaxis((codes * scale).reshape(v.shape), -1, axis)


WIDE = False


def mx_kscale(k):
    if not WIDE:
        return np.ones(k)
    levels = np.array([10, -10, 5, -5, 0])
    if k % 512:
        return np.exp2(np.random.permutation(np.resize(levels, k // 32))).repeat(32)
    a = np.empty((k // 512, 16))
    for p in range(k // 512):
        a[p, :8] = np.random.permutation(np.resize(levels, 8))
        for g in range(8):
            far = levels[np.abs(levels - a[p, g]) >= 10]
            a[p, g + 8] = far[np.random.randint(len(far))]
    return np.exp2(a.ravel()).repeat(32)


def f64(x):
    return np.asarray(x).astype(np.float64)


def striped(idx):
    return np.tile(idx.reshape(-1, 16).T, (8, 1)).astype(np.uint16)


def unstriped(offs):
    return offs[:16].T.reshape(-1).astype(np.int64)


def striped8(idx):
    return np.concatenate([x.reshape(-1, 16).T for x in idx]).astype(np.uint16)


def runs(offs, k):
    lists = np.stack([offs[16 * r : 16 * r + 16].T.reshape(-1) for r in range(8)]).astype(np.int64)
    return lists[np.arange(k) % 512 // 64]


def pack_weight(w):
    k, n = w.shape
    w = f64(np.asarray(w, np.float32).astype(ml_dtypes.bfloat16)).reshape(k // 32, 32, n)
    amax = np.abs(w).max(1)
    byte = np.clip(np.where(amax > 0, np.frexp(amax)[1] - 1 + 127 - 7, 1), 1, 254)
    scaled = (w * np.exp2(127.0 - byte)[:, None, :]).reshape(k, n).astype(np.float32)
    words = np.ascontiguousarray(scaled.reshape(k // 512, 128, 4, n).transpose(0, 1, 3, 2)).astype(ml_dtypes.float8_e4m3fn).view(np.uint8)
    return words, np.ascontiguousarray(byte.astype(np.uint8).reshape(k // 512, 16, n))


def unpack_weight(words, scales):
    g, p, n, _ = words.shape
    vals = np.ascontiguousarray(words).view(ml_dtypes.float8_e4m3fn).astype(np.float64) * np.repeat(np.exp2(scales.astype(np.float64) - 127.0), 8, axis=1)[..., None]
    return vals.transpose(0, 1, 3, 2).reshape(g * 512, n)


def sigmoid(v):
    return 1.0 / (1.0 + np.exp(-np.maximum(v, -700.0)))


K, T, S, N, G, H = 512, 2048, 256, 512, 2048, 512


def setup_inputs():
    n = np.random.standard_normal
    s = mx_kscale(K)[:, None]
    u = mx_kscale(K)
    packed_xT = pack_weight(n((K, T)) * s)
    packed_dT = pack_weight(n((K, G)) / s)
    return {
        "x_words": packed_xT[0],
        "x_scales": packed_xT[1],
        "d_words": packed_dT[0],
        "d_scales": packed_dT[1],
        "gn": (np.random.uniform(0.5, 1.5, (H, 1)) * u[:, None]).astype(np.float32),
        "w1": (n((H, N)) / np.sqrt(2 * H) / u[:, None]).astype(np.float32),
        "w2": (n((K, N)) / np.sqrt(2 * K) / s).astype(np.float32),
        "sl": np.random.uniform(1.0, 2.0, (N, 1)).astype(np.float32),
        "th": (0.5 * n((N, 1))).astype(np.float32),
        "offs": striped(np.random.permutation(T)[:S]),
        "k1": striped8(np.random.randint(0, G, (8, H))),
        "two": striped(np.random.permutation(T)[:S]),
        "n1": striped(np.random.permutation(S)),
        "n2": striped(np.random.permutation(S)),
    }


def reference(x_words, x_scales, d_words, d_scales, gn, w1, w2, sl, th, offs, k1, two, n1, n2):
    d_k1 = unpack_weight(d_words, d_scales)[np.arange(K)[:, None], runs(k1, K)]
    xq = unpack_weight(x_words, x_scales)[:, unstriped(offs)]
    s = 0.0625 * (d_k1.T @ xq)
    z = f64(gn) * s
    x_two = unpack_weight(x_words, x_scales)[:, unstriped(two)]
    h = mxq(f64(w1), 0, "e4m3").T @ mxq(z, 0, "e4m3") + mxq(f64(w2), 0, "e4m3").T @ x_two
    ds = np.zeros((N, S))
    ds[:, unstriped(n1)] = h
    sg = sigmoid(f64(sl) * (ds[:, unstriped(n2)] - f64(th)))
    return h * sg

@@ -1,0 +1,214 @@
+from contextlib import ExitStack
+
+import concourse.mybir as mybir
+
+K, T, S, N, G, H = 512, 2048, 256, 512, 2048, 512
+FLOPS = 2 * S * (K * H + H * N + K * N)
+
+F32 = mybir.dt.float32
+BF16 = mybir.dt.bfloat16
+I32 = mybir.dt.int32
+U32 = mybir.dt.uint32
+U16 = mybir.dt.uint16
+U8 = mybir.dt.uint8
+FP8X4 = mybir.dt.float8_e4m3fn_x4
+ALU = mybir.AluOpType
+ACT = mybir.ActivationFunctionType
+
+P = 128
+PACK = 4
+HALF = S // 2
+TILES = N // P
+WINDOW = 2 * S
+W_CHUNKS = ((0, 1), (1, 2), (2, 4))
+AT_D_BYTES = 1024
+AT_X_BYTES = 4096
+AT_KEY_WORDS = AT_X_BYTES + 2048 + 3072
+AT_D_TABLE = AT_KEY_WORDS + 5120
+AT_W_RAW = ((0, 2048), (AT_D_TABLE, AT_D_TABLE + 2048), (AT_KEY_WORDS - 3072, AT_KEY_WORDS + 1024))
+
+
+def tile_picked_kmixierl_none_p_kernel(
+    tc, x_words, x_scales, d_words, d_scales, gn, w1, w2, sl, th, offs, k1, two, n1, n2, out
+):
+    nc = tc.nc
+    with ExitStack() as ctx:
+        sb = ctx.enter_context(tc.tile_pool(name="sb", bufs=1))
+        reuse = ctx.enter_context(tc.tile_pool(name="reuse", bufs=1))
+        psum = ctx.enter_context(tc.psum_pool(name="psum", bufs=1))
+
+        def load_list(src, name):
+            t = sb.tile(list(src.shape), U16, name=name)
+            nc.sync.dma_start(t[:], src)
+            return t
+
+        def load_words(t, src):
+            nc.sync.dma_start(t[:].bitcast(I32), src[0].rearrange("p n r -> p (n r)").bitcast(I32))
+
+        d_bytes = reuse.tile([P, G], U8, name="d_bytes", offset=AT_D_BYTES, align_bytes=64)
+        x_bytes = reuse.tile([P, T], U8, name="x_bytes", offset=AT_X_BYTES, align_bytes=64)
+        nc.vector.memset(x_bytes[:].bitcast(I32), 0)
+
+        k1_sb = load_list(k1, "k1_sb")
+        nc.sync.dma_start(
+            d_bytes[:].bitcast(I32), d_scales[0].bitcast(I32).unsqueeze(1).to_broadcast([16, 8, G // 4])
+        )
+        offs_sb = load_list(offs, "offs_sb")
+        two_sb = load_list(two, "two_sb")
+        n1_sb = load_list(n1, "n1_sb")
+        n2_sb = load_list(n2, "n2_sb")
+        d_table = reuse.tile([P, G], U32, name="d_table", offset=AT_D_TABLE, align_bytes=64)
+        x_table = sb.tile([P, T], U32, name="x_table")
+        load_words(d_table, d_words)
+        load_words(x_table, x_words)
+        for q in range(4):
+            nc.scalar.dma_start(
+                x_bytes[32 * q : 32 * q + 4, :].bitcast(I32), x_scales[0, 4 * q : 4 * q + 4, :].bitcast(I32)
+            )
+
+        gn_sb = sb.tile([P, PACK], F32, name="gn_sb")
+        sl_sb = sb.tile([P, TILES], F32, name="sl_sb")
+        th_sb = sb.tile([P, TILES], F32, name="th_sb")
+        nc.gpsimd.dma_start(gn_sb[:], gn.rearrange("(p t) o -> p (t o)", t=PACK))
+        with nc.allow_non_contiguous_dma(reason="one value a row"):
+            nc.gpsimd.dma_start(sl_sb[:], sl.rearrange("(m p) o -> p (m o)", p=P))
+            nc.gpsimd.dma_start(th_sb[:], th.rearrange("(m p) o -> p (m o)", p=P))
+
+        raw = {}
+
+        def load_weights(chunk):
+            lo, hi = W_CHUNKS[chunk]
+            for a, (name, w) in enumerate((("w2", w2), ("w1", w1))):
+                at = AT_W_RAW[chunk][a]
+                t = reuse.tile([P, PACK, (hi - lo) * P], F32, name=f"{name}_raw{chunk}", offset=at, align_bytes=64)
+                src = w[:, lo * P : hi * P].rearrange("(p j) c -> p j c", j=PACK)
+                if chunk == 0:
+                    nc.sync.dma_start(t[:, 0:2], src[:, 0:2])
+                    nc.sync.dma_start(t[:, 2:4], src[:, 2:4])
+                else:
+                    nc.sync.dma_start(t[:], src)
+                for m in range(lo, hi):
+                    raw[name, m] = t[:, :, (m - lo) * P : (m - lo + 1) * P]
+
+        key_bytes = sb.tile([P, H], U8, name="key_bytes")
+        nc.vector.tensor_copy(key_bytes[:], d_bytes[:].indirect(k1_sb[:]))
+        load_weights(0)
+        key_scale = sb.tile([P, H], U8, name="key_scale", align_bytes=64)
+        nc.vector.tensor_copy(
+            key_scale[:].rearrange("p (t m) -> p t m", t=PACK), key_bytes[:].rearrange("p (m t) -> p t m", t=PACK)
+        )
+        for c in range(1, 4):
+            nc.scalar.dma_start(key_scale[c:P:32, :].bitcast(I32), key_scale[8 * c : P : 32, :].bitcast(I32))
+
+        key_words = reuse.tile([P, H], U32, name="key_words", offset=AT_KEY_WORDS, align_bytes=64)
+        nc.vector.tensor_copy(key_words[:], d_table[:].indirect(k1_sb[:]))
+        load_weights(1)
+        key_codes = sb.tile([P, H], U32, name="key_codes", align_bytes=64)
+        nc.vector.tensor_copy(
+            key_codes[:].bitcast(I32).rearrange("p (t m) -> p t m", t=PACK),
+            key_words[:].bitcast(I32).rearrange("p (m t) -> p t m", t=PACK),
+        )
+
+        load_weights(2)
+
+        xq_scale = sb.tile([P, S], U8, name="xq_scale", align_bytes=64)
+        x2_scale = sb.tile([P, S], U8, name="x2_scale", align_bytes=64)
+        nc.vector.tensor_copy(xq_scale[:], x_bytes[:].indirect(offs_sb[:]))
+        nc.vector.tensor_copy(x2_scale[:], x_bytes[:].indirect(two_sb[:]))
+        xq_codes = reuse.tile([P, S], U32, name="xq_codes", offset=AT_X_BYTES, align_bytes=64)
+        x2_codes = reuse.tile([P, S], U32, name="x2_codes", offset=AT_X_BYTES + 4 * S, align_bytes=64)
+        nc.vector.tensor_copy(xq_codes[:], x_table[:].indirect(offs_sb[:]))
+        nc.vector.tensor_copy(x2_codes[:], x_table[:].indirect(two_sb[:]))
+
+        z_bf = sb.tile([P, S, PACK], BF16, name="z_bf", align_bytes=64)
+        z_codes = sb.tile([P, S], U32, name="z_codes", align_bytes=64)
+        z_scale = sb.tile([P, S], U8, name="z_scale", align_bytes=64)
+        for u in range(2):
+            cols = slice(u * HALF, (u + 1) * HALF)
+            s_ps = psum.tile([P, PACK, HALF], F32, name=f"s_ps{u}")
+            for t in range(PACK):
+                keys = slice(t * P, (t + 1) * P)
+                nc.tensor.matmul_mx(
+                    out=s_ps[:, t, :],
+                    lhsT=key_codes[:, keys].bitcast(FP8X4),
+                    lhsT_scale=key_scale[:, keys],
+                    rhs=xq_codes[:, cols].bitcast(FP8X4),
+                    rhs_scale=xq_scale[:, cols],
+                    start=True,
+                    stop=True,
+                )
+            nc.vector.scalar_tensor_tensor(
+                z_bf[:, cols, :],
+                s_ps[:].rearrange("p t j -> p j t"),
+                0.0625,
+                gn_sb[:].unsqueeze(1).to_broadcast([P, HALF, PACK]),
+                ALU.mult,
+                ALU.mult,
+            )
+
+        w_codes, w_scale = {}, {}
+
+        def quantize_weights(m):
+            w_bf = sb.tile([P, 2, P, PACK], BF16, name=f"w_bf{m}", align_bytes=64)
+            for a, name in enumerate(("w2", "w1")):
+                src = raw[name, m].rearrange("p j c -> p c j")
+                if m == 0:
+                    nc.scalar.copy(w_bf[:, a], src)
+                else:
+                    nc.vector.tensor_copy(w_bf[:, a], src)
+            w_codes[m] = sb.tile([P, 2 * P], U32, name=f"w_codes{m}", align_bytes=64)
+            w_scale[m] = sb.tile([P, 2 * P], U8, name=f"w_scale{m}", align_bytes=64)
+            nc.vector.quantize_mx(
+                out=w_codes[m][:].bitcast(FP8X4), scales=w_scale[m][:], in_=w_bf[:].rearrange("p a c j -> p (a c j)")
+            )
+
+        quantize_weights(0)
+        nc.vector.quantize_mx(
+            out=z_codes[:].bitcast(FP8X4), scales=z_scale[:], in_=z_bf[:].rearrange("p j t -> p (j t)")
+        )
+
+        h_sb, ds, sg = {}, {}, {}
+
+        def product(m):
+            h_ps = psum.tile([P, S], F32, name=f"h_ps{m}")
+            for a, (codes, scale) in enumerate(((x2_codes, x2_scale), (z_codes, z_scale))):
+                cols = slice(a * P, (a + 1) * P)
+                nc.tensor.matmul_mx(
+                    out=h_ps[:],
+                    lhsT=w_codes[m][:, cols].bitcast(FP8X4),
+                    lhsT_scale=w_scale[m][:, cols],
+                    rhs=codes[:].bitcast(FP8X4),
+                    rhs_scale=scale[:],
+                    start=(a == 0),
+                    stop=(a == 1),
+                )
+            h_sb[m] = sb.tile([P, S], F32, name=f"h_sb{m}")
+            if m == 0:
+                nc.scalar.copy(h_sb[m][:], h_ps[:])
+            else:
+                nc.vector.tensor_copy(h_sb[m][:], h_ps[:])
+
+        def scatter(m):
+            ds[m] = sb.tile([P, WINDOW], F32, name=f"ds{m}")
+            nc.scalar.activation(ds[m][:].indirect(n1_sb[:]), h_sb[m][:], ACT.Copy)
+
+        def finish(m):
+            sg[m] = sb.tile([P, S], F32, name=f"sg{m}")
+            nc.scalar.activation(
+                sg[m][:], ds[m][:].indirect(n2_sb[:]), ACT.Sigmoid, bias=bias[:, m : m + 1], scale=sl_sb[:, m : m + 1]
+            )
+            res = sb.tile([P, S], F32, name=f"res{m}")
+            (nc.gpsimd if m < 2 else nc.vector).tensor_tensor(res[:], h_sb[m][:], sg[m][:], ALU.mult)
+            nc.sync.dma_start(out[m * P : (m + 1) * P, :], res[:])
+
+        bias = sb.tile([P, TILES], F32, name="bias")
+        for m in range(TILES):
+            if m > 0:
+                quantize_weights(m)
+            else:
+                nc.vector.scalar_tensor_tensor(bias[:], sl_sb[:], -1.0, th_sb[:], ALU.mult, ALU.mult)
+            product(m)
+            scatter(m)
+            if m > 0:
+                finish(m - 1)
+        finish(TILES - 1)

@@ -21,11 +21,6 @@ HALF = S // 2
 TILES = N // P
 WINDOW = 2 * S
 W_CHUNKS = ((0, 1), (1, 2), (2, 4))
-AT_D_BYTES = 1024
-AT_X_BYTES = 4096
-AT_KEY_WORDS = AT_X_BYTES + 2048 + 3072
-AT_D_TABLE = AT_KEY_WORDS + 5120
-AT_W_RAW = ((0, 2048), (AT_D_TABLE, AT_D_TABLE + 2048), (AT_KEY_WORDS - 3072, AT_KEY_WORDS + 1024))
 
 
 def tile_picked_kmixierl_none_p_kernel(
@@ -42,94 +37,98 @@ def tile_picked_kmixierl_none_p_kernel(
             nc.sync.dma_start(t[:], src)
             return t
 
-        def load_words(t, src):
+        def load_words(src, name):
+            t = sb.tile([P, src.shape[2]], U32, name=name)
             nc.sync.dma_start(t[:].bitcast(I32), src[0].rearrange("p n r -> p (n r)").bitcast(I32))
+            return t
 
-        d_bytes = reuse.tile([P, G], U8, name="d_bytes", offset=AT_D_BYTES, align_bytes=64)
-        x_bytes = reuse.tile([P, T], U8, name="x_bytes", offset=AT_X_BYTES, align_bytes=64)
-        nc.vector.memset(x_bytes[:].bitcast(I32), 0)
+        d_bytes = sb.tile([P, G], U8, name="d_bytes")
+        x_bytes = reuse.tile([P, T], U8, name="x_bytes", offset=1024)
+        nc.vector.memset(d_bytes[:].bitcast(I32), 0)
 
         k1_sb = load_list(k1, "k1_sb")
-        nc.sync.dma_start(
-            d_bytes[:].bitcast(I32), d_scales[0].bitcast(I32).unsqueeze(1).to_broadcast([16, 8, G // 4])
-        )
+        x_rows = x_scales[0].bitcast(I32).rearrange("(q c) n -> c q n", c=4)
+        for c in range(4):
+            nc.scalar.dma_start(x_bytes[c:P:4, :].bitcast(I32), x_rows[c].unsqueeze(1).to_broadcast([4, 8, T // 4]))
+        nc.sync.dma_start(d_bytes[0:P:8, :].bitcast(I32), d_scales[0].bitcast(I32))
         offs_sb = load_list(offs, "offs_sb")
+        d_table = load_words(d_words, "d_table")
         two_sb = load_list(two, "two_sb")
-        n1_sb = load_list(n1, "n1_sb")
-        n2_sb = load_list(n2, "n2_sb")
-        d_table = reuse.tile([P, G], U32, name="d_table", offset=AT_D_TABLE, align_bytes=64)
-        x_table = sb.tile([P, T], U32, name="x_table")
-        load_words(d_table, d_words)
-        load_words(x_table, x_words)
-        for q in range(4):
-            nc.scalar.dma_start(
-                x_bytes[32 * q : 32 * q + 4, :].bitcast(I32), x_scales[0, 4 * q : 4 * q + 4, :].bitcast(I32)
-            )
+        x_table = load_words(x_words, "x_table")
 
         gn_sb = sb.tile([P, PACK], F32, name="gn_sb")
         sl_sb = sb.tile([P, TILES], F32, name="sl_sb")
         th_sb = sb.tile([P, TILES], F32, name="th_sb")
         nc.gpsimd.dma_start(gn_sb[:], gn.rearrange("(p t) o -> p (t o)", t=PACK))
-        with nc.allow_non_contiguous_dma(reason="one value a row"):
-            nc.gpsimd.dma_start(sl_sb[:], sl.rearrange("(m p) o -> p (m o)", p=P))
-            nc.gpsimd.dma_start(th_sb[:], th.rearrange("(m p) o -> p (m o)", p=P))
 
         raw = {}
 
         def load_weights(chunk):
             lo, hi = W_CHUNKS[chunk]
-            for a, (name, w) in enumerate((("w2", w2), ("w1", w1))):
-                at = AT_W_RAW[chunk][a]
-                t = reuse.tile([P, PACK, (hi - lo) * P], F32, name=f"{name}_raw{chunk}", offset=at, align_bytes=64)
-                src = w[:, lo * P : hi * P].rearrange("(p j) c -> p j c", j=PACK)
+            for name, w in (("w2", w2), ("w1", w1)):
                 if chunk == 0:
-                    nc.sync.dma_start(t[:, 0:2], src[:, 0:2])
-                    nc.sync.dma_start(t[:, 2:4], src[:, 2:4])
+                    t = reuse.tile([P, PACK, P], F32, name=f"{name}_raw0", offset={"w1": 2048, "w2": 4096}[name])
                 else:
-                    nc.sync.dma_start(t[:], src)
+                    t = sb.tile([P, PACK, (hi - lo) * P], F32, name=f"{name}_raw{chunk}")
+                nc.sync.dma_start(t[:], w[:, lo * P : hi * P].rearrange("(p j) c -> p j c", j=PACK))
                 for m in range(lo, hi):
                     raw[name, m] = t[:, :, (m - lo) * P : (m - lo + 1) * P]
 
-        key_bytes = sb.tile([P, H], U8, name="key_bytes")
+
+        key_bytes = reuse.tile([P, H], U8, name="key_bytes", offset=4096)
         nc.vector.tensor_copy(key_bytes[:], d_bytes[:].indirect(k1_sb[:]))
-        load_weights(0)
         key_scale = sb.tile([P, H], U8, name="key_scale", align_bytes=64)
         nc.vector.tensor_copy(
-            key_scale[:].rearrange("p (t m) -> p t m", t=PACK), key_bytes[:].rearrange("p (m t) -> p t m", t=PACK)
+            key_scale[:].rearrange("p (t c i) -> p c t i", t=PACK, i=16),
+            key_bytes[:].rearrange("p (c i t) -> p c t i", t=PACK, i=16),
         )
         for c in range(1, 4):
             nc.scalar.dma_start(key_scale[c:P:32, :].bitcast(I32), key_scale[8 * c : P : 32, :].bitcast(I32))
-
-        key_words = reuse.tile([P, H], U32, name="key_words", offset=AT_KEY_WORDS, align_bytes=64)
-        nc.vector.tensor_copy(key_words[:], d_table[:].indirect(k1_sb[:]))
-        load_weights(1)
-        key_codes = sb.tile([P, H], U32, name="key_codes", align_bytes=64)
-        nc.vector.tensor_copy(
-            key_codes[:].bitcast(I32).rearrange("p (t m) -> p t m", t=PACK),
-            key_words[:].bitcast(I32).rearrange("p (m t) -> p t m", t=PACK),
-        )
-
-        load_weights(2)
 
         xq_scale = sb.tile([P, S], U8, name="xq_scale", align_bytes=64)
         x2_scale = sb.tile([P, S], U8, name="x2_scale", align_bytes=64)
         nc.vector.tensor_copy(xq_scale[:], x_bytes[:].indirect(offs_sb[:]))
         nc.vector.tensor_copy(x2_scale[:], x_bytes[:].indirect(two_sb[:]))
-        xq_codes = reuse.tile([P, S], U32, name="xq_codes", offset=AT_X_BYTES, align_bytes=64)
-        x2_codes = reuse.tile([P, S], U32, name="x2_codes", offset=AT_X_BYTES + 4 * S, align_bytes=64)
-        nc.vector.tensor_copy(xq_codes[:], x_table[:].indirect(offs_sb[:]))
-        nc.vector.tensor_copy(x2_codes[:], x_table[:].indirect(two_sb[:]))
 
-        z_bf = sb.tile([P, S, PACK], BF16, name="z_bf", align_bytes=64)
+        load_weights(0)
+        n1_sb = load_list(n1, "n1_sb")
+        load_weights(1)
+        n2_sb = load_list(n2, "n2_sb")
+        with nc.allow_non_contiguous_dma(reason="one value a row"):
+            nc.sync.dma_start(sl_sb[:], sl.rearrange("(m p) o -> p (m o)", p=P))
+            nc.sync.dma_start(th_sb[:], th.rearrange("(m p) o -> p (m o)", p=P))
+        load_weights(2)
+
+        key_words = reuse.tile([P, H], U32, name="key_words", offset=0)
+        nc.vector.tensor_copy(key_words[:], d_table[:].indirect(k1_sb[:]))
+        key_codes = sb.tile([P, H], U32, name="key_codes", align_bytes=64)
+        nc.vector.tensor_copy(
+            key_codes[:].bitcast(I32).rearrange("p (t c i) -> p c t i", t=PACK, i=4),
+            key_words[:].bitcast(I32).rearrange("p (c i t) -> p c t i", t=PACK, i=4),
+        )
+
+        xq_codes = sb.tile([P, S], U32, name="xq_codes", align_bytes=64)
+        x2_codes = sb.tile([P, S], U32, name="x2_codes", align_bytes=64)
+        z_bf = {}
         z_codes = sb.tile([P, S], U32, name="z_codes", align_bytes=64)
         z_scale = sb.tile([P, S], U8, name="z_scale", align_bytes=64)
-        for u in range(2):
-            cols = slice(u * HALF, (u + 1) * HALF)
-            s_ps = psum.tile([P, PACK, HALF], F32, name=f"s_ps{u}")
+
+        def columns(u):
+            return slice(u * HALF, (u + 1) * HALF)
+
+        def entries(u):
+            return slice(u * HALF // 16, (u + 1) * HALF // 16)
+
+        s_ps = {}
+
+        def score(u):
+            cols = columns(u)
+            nc.vector.tensor_copy(xq_codes[:, cols], x_table[:].indirect(offs_sb[:, entries(u)]))
+            s_ps[u] = psum.tile([P, PACK, HALF], F32, name=f"s_ps{u}")
             for t in range(PACK):
                 keys = slice(t * P, (t + 1) * P)
                 nc.tensor.matmul_mx(
-                    out=s_ps[:, t, :],
+                    out=s_ps[u][:, t, :],
                     lhsT=key_codes[:, keys].bitcast(FP8X4),
                     lhsT_scale=key_scale[:, keys],
                     rhs=xq_codes[:, cols].bitcast(FP8X4),
@@ -137,78 +136,98 @@ def tile_picked_kmixierl_none_p_kernel(
                     start=True,
                     stop=True,
                 )
+
+        def pick_two(u):
+            nc.vector.tensor_copy(x2_codes[:, columns(u)], x_table[:].indirect(two_sb[:, entries(u)]))
+
+        def make_z(u):
+            z_bf[u] = sb.tile([P, HALF, PACK], BF16, name=f"z_bf{u}", tag=("z_bf0", "w_bf0")[u], align_bytes=64)
             nc.vector.scalar_tensor_tensor(
-                z_bf[:, cols, :],
-                s_ps[:].rearrange("p t j -> p j t"),
+                z_bf[u][:],
+                s_ps[u][:].rearrange("p t j -> p j t"),
                 0.0625,
                 gn_sb[:].unsqueeze(1).to_broadcast([P, HALF, PACK]),
                 ALU.mult,
                 ALU.mult,
             )
 
+        def quantize_z(u):
+            nc.vector.quantize_mx(
+                out=z_codes[:, columns(u)].bitcast(FP8X4),
+                scales=z_scale[:, columns(u)],
+                in_=z_bf[u][:].rearrange("p j t -> p (j t)"),
+            )
+
         w_codes, w_scale = {}, {}
 
         def quantize_weights(m):
-            w_bf = sb.tile([P, 2, P, PACK], BF16, name=f"w_bf{m}", align_bytes=64)
+            w_bf = sb.tile([P, 2, P, PACK], BF16, name=f"w_bf{m}", tag=f"w_bf{m}", align_bytes=64)
             for a, name in enumerate(("w2", "w1")):
-                src = raw[name, m].rearrange("p j c -> p c j")
-                if m == 0:
-                    nc.scalar.copy(w_bf[:, a], src)
-                else:
-                    nc.vector.tensor_copy(w_bf[:, a], src)
+                copy = nc.scalar.copy if m == 0 else nc.vector.tensor_copy
+                copy(
+                    w_bf[:, a].rearrange("p (c i) j -> p c j i", i=4), raw[name, m].rearrange("p j (c i) -> p c j i", i=4)
+                )
             w_codes[m] = sb.tile([P, 2 * P], U32, name=f"w_codes{m}", align_bytes=64)
             w_scale[m] = sb.tile([P, 2 * P], U8, name=f"w_scale{m}", align_bytes=64)
             nc.vector.quantize_mx(
                 out=w_codes[m][:].bitcast(FP8X4), scales=w_scale[m][:], in_=w_bf[:].rearrange("p a c j -> p (a c j)")
             )
 
-        quantize_weights(0)
-        nc.vector.quantize_mx(
-            out=z_codes[:].bitcast(FP8X4), scales=z_scale[:], in_=z_bf[:].rearrange("p j t -> p (j t)")
-        )
+        minus_sl = sb.tile([P, TILES], F32, name="minus_sl")
+        bias = sb.tile([P, TILES], F32, name="bias")
+        nc.gpsimd.tensor_scalar(minus_sl[:], sl_sb[:], -1.0, 0.0, ALU.mult, ALU.add)
+        nc.gpsimd.tensor_tensor(bias[:], minus_sl[:], th_sb[:], ALU.mult)
 
-        h_sb, ds, sg = {}, {}, {}
+        h_sb = [sb.tile([P, S], F32, name=f"h_sb{m}") for m in range(TILES)]
+        ds = [sb.tile([P, WINDOW], F32, name=f"ds{m}") for m in range(TILES)]
+        sg = [sb.tile([P, S], F32, name=f"sg{m}") for m in range(TILES)]
+        res = [sb.tile([P, S], F32, name=f"res{m}") for m in range(TILES)]
 
-        def product(m):
-            h_ps = psum.tile([P, S], F32, name=f"h_ps{m}")
+        def product(m, cols, evacuate):
+            h_ps = psum.tile([P, cols.stop - cols.start], F32, name=f"h_ps{m}_{cols.start}")
             for a, (codes, scale) in enumerate(((x2_codes, x2_scale), (z_codes, z_scale))):
-                cols = slice(a * P, (a + 1) * P)
+                rows = slice(a * P, (a + 1) * P)
                 nc.tensor.matmul_mx(
                     out=h_ps[:],
-                    lhsT=w_codes[m][:, cols].bitcast(FP8X4),
-                    lhsT_scale=w_scale[m][:, cols],
-                    rhs=codes[:].bitcast(FP8X4),
-                    rhs_scale=scale[:],
+                    lhsT=w_codes[m][:, rows].bitcast(FP8X4),
+                    lhsT_scale=w_scale[m][:, rows],
+                    rhs=codes[:, cols].bitcast(FP8X4),
+                    rhs_scale=scale[:, cols],
                     start=(a == 0),
                     stop=(a == 1),
                 )
-            h_sb[m] = sb.tile([P, S], F32, name=f"h_sb{m}")
-            if m == 0:
-                nc.scalar.copy(h_sb[m][:], h_ps[:])
-            else:
-                nc.vector.tensor_copy(h_sb[m][:], h_ps[:])
+            evacuate(h_sb[m][:, cols], h_ps[:])
 
-        def scatter(m):
-            ds[m] = sb.tile([P, WINDOW], F32, name=f"ds{m}")
-            nc.scalar.activation(ds[m][:].indirect(n1_sb[:]), h_sb[m][:], ACT.Copy)
+        def scatter(m, cols):
+            listed = n1_sb[:, cols.start // 16 : cols.stop // 16]
+            nc.scalar.activation(ds[m][:].indirect(listed), h_sb[m][:, cols], ACT.Copy)
 
-        def finish(m):
-            sg[m] = sb.tile([P, S], F32, name=f"sg{m}")
+        def finish(m, cols, engine):
+            listed = n2_sb[:, cols.start // 16 : cols.stop // 16]
             nc.scalar.activation(
-                sg[m][:], ds[m][:].indirect(n2_sb[:]), ACT.Sigmoid, bias=bias[:, m : m + 1], scale=sl_sb[:, m : m + 1]
+                sg[m][:, cols], ds[m][:].indirect(listed), ACT.Sigmoid, bias=bias[:, m : m + 1], scale=sl_sb[:, m : m + 1]
             )
-            res = sb.tile([P, S], F32, name=f"res{m}")
-            (nc.gpsimd if m < 2 else nc.vector).tensor_tensor(res[:], h_sb[m][:], sg[m][:], ALU.mult)
-            nc.sync.dma_start(out[m * P : (m + 1) * P, :], res[:])
+            engine.tensor_tensor(res[m][:, cols], h_sb[m][:, cols], sg[m][:, cols], ALU.mult)
+            nc.sync.dma_start(out[m * P : (m + 1) * P, cols], res[m][:, cols])
 
-        bias = sb.tile([P, TILES], F32, name="bias")
-        for m in range(TILES):
-            if m > 0:
-                quantize_weights(m)
-            else:
-                nc.vector.scalar_tensor_tensor(bias[:], sl_sb[:], -1.0, th_sb[:], ALU.mult, ALU.mult)
-            product(m)
-            scatter(m)
-            if m > 0:
-                finish(m - 1)
-        finish(TILES - 1)
+        score(0)
+        pick_two(0)
+        score(1)
+        make_z(0)
+        pick_two(1)
+        quantize_z(0)
+        quantize_weights(0)
+        product(0, columns(0), nc.scalar.copy)
+        scatter(0, columns(0))
+        make_z(1)
+        quantize_z(1)
+        product(0, columns(1), nc.scalar.copy)
+        scatter(0, columns(1))
+        every = slice(0, S)
+        for m in range(1, TILES):
+            quantize_weights(m)
+            product(m, every, nc.vector.tensor_copy)
+            scatter(m, every)
+            finish(m - 1, every, nc.gpsimd)
+        for u in range(2):
+            finish(TILES - 1, columns(u), nc.vector)

@@ -1,6 +1,7 @@
 from contextlib import ExitStack
 
 import concourse.mybir as mybir
+from concourse.masks import make_identity
 
 K, T, S, N, G, H = 512, 2048, 256, 512, 2048, 512
 FLOPS = 2 * S * (K * H + H * N + K * N)
@@ -29,7 +30,6 @@ def tile_picked_kmixierl_none_p_kernel(
     nc = tc.nc
     with ExitStack() as ctx:
         sb = ctx.enter_context(tc.tile_pool(name="sb", bufs=1))
-        reuse = ctx.enter_context(tc.tile_pool(name="reuse", bufs=1))
         psum = ctx.enter_context(tc.psum_pool(name="psum", bufs=1))
 
         def load_list(src, name):
@@ -43,39 +43,48 @@ def tile_picked_kmixierl_none_p_kernel(
             return t
 
         d_bytes = sb.tile([P, G], U8, name="d_bytes")
-        x_bytes = reuse.tile([P, T], U8, name="x_bytes", offset=1024)
+        x_bytes = sb.tile([P, T], U8, name="x_bytes")
         nc.vector.memset(d_bytes[:].bitcast(I32), 0)
+        nc.vector.memset(x_bytes[:].bitcast(I32), 0)
 
         k1_sb = load_list(k1, "k1_sb")
-        x_rows = x_scales[0].bitcast(I32).rearrange("(q c) n -> c q n", c=4)
-        for c in range(4):
-            nc.scalar.dma_start(x_bytes[c:P:4, :].bitcast(I32), x_rows[c].unsqueeze(1).to_broadcast([4, 8, T // 4]))
+        for q in range(4):
+            nc.scalar.dma_start(
+                x_bytes[32 * q : 32 * q + 4, :].bitcast(I32), x_scales[0, 4 * q : 4 * q + 4, :].bitcast(I32)
+            )
         nc.sync.dma_start(d_bytes[0:P:8, :].bitcast(I32), d_scales[0].bitcast(I32))
         offs_sb = load_list(offs, "offs_sb")
         d_table = load_words(d_words, "d_table")
         two_sb = load_list(two, "two_sb")
+        n1_sb = load_list(n1, "n1_sb")
+        n2_sb = load_list(n2, "n2_sb")
         x_table = load_words(x_words, "x_table")
 
         gn_sb = sb.tile([P, PACK], F32, name="gn_sb")
-        sl_sb = sb.tile([P, TILES], F32, name="sl_sb")
-        th_sb = sb.tile([P, TILES], F32, name="th_sb")
         nc.gpsimd.dma_start(gn_sb[:], gn.rearrange("(p t) o -> p (t o)", t=PACK))
+        warm_out = sb.tile([P, 1], F32, name="warm_out")
+        nc.scalar.activation(warm_out[:], gn_sb[:, 0:1], ACT.Sigmoid)
+        gate_rows = sb.tile([P, P], F32, name="gate_rows")
+        identity = sb.tile([P, P], F32, name="identity")
+        nc.gpsimd.memset(gate_rows[:], 0.0)
+        nc.gpsimd.dma_start(gate_rows[0:TILES, :], sl.rearrange("(m p) o -> m (p o)", p=P))
+        nc.gpsimd.dma_start(gate_rows[TILES : 2 * TILES, :], th.rearrange("(m p) o -> m (p o)", p=P))
+        make_identity(nc, identity[:])
 
         raw = {}
 
-        def load_weights(chunk):
+        def load_weights(name, w, chunk):
             lo, hi = W_CHUNKS[chunk]
-            for name, w in (("w2", w2), ("w1", w1)):
-                if chunk == 0:
-                    t = reuse.tile([P, PACK, P], F32, name=f"{name}_raw0", offset={"w1": 2048, "w2": 4096}[name])
-                else:
-                    t = sb.tile([P, PACK, (hi - lo) * P], F32, name=f"{name}_raw{chunk}")
-                nc.sync.dma_start(t[:], w[:, lo * P : hi * P].rearrange("(p j) c -> p j c", j=PACK))
-                for m in range(lo, hi):
-                    raw[name, m] = t[:, :, (m - lo) * P : (m - lo + 1) * P]
+            t = sb.tile([P, PACK, (hi - lo) * P], F32, name=f"{name}_raw{chunk}")
+            nc.sync.dma_start(t[:], w[:, lo * P : hi * P].rearrange("(p j) c -> p j c", j=PACK))
+            for m in range(lo, hi):
+                raw[name, m] = t[:, :, (m - lo) * P : (m - lo + 1) * P]
 
+        for chunk in range(len(W_CHUNKS)):
+            load_weights("w2", w2, chunk)
+            load_weights("w1", w1, chunk)
 
-        key_bytes = reuse.tile([P, H], U8, name="key_bytes", offset=4096)
+        key_bytes = sb.tile([P, H], U8, name="key_bytes")
         nc.vector.tensor_copy(key_bytes[:], d_bytes[:].indirect(k1_sb[:]))
         key_scale = sb.tile([P, H], U8, name="key_scale", align_bytes=64)
         nc.vector.tensor_copy(
@@ -85,27 +94,18 @@ def tile_picked_kmixierl_none_p_kernel(
         for c in range(1, 4):
             nc.scalar.dma_start(key_scale[c:P:32, :].bitcast(I32), key_scale[8 * c : P : 32, :].bitcast(I32))
 
-        xq_scale = sb.tile([P, S], U8, name="xq_scale", align_bytes=64)
-        x2_scale = sb.tile([P, S], U8, name="x2_scale", align_bytes=64)
-        nc.vector.tensor_copy(xq_scale[:], x_bytes[:].indirect(offs_sb[:]))
-        nc.vector.tensor_copy(x2_scale[:], x_bytes[:].indirect(two_sb[:]))
 
-        load_weights(0)
-        n1_sb = load_list(n1, "n1_sb")
-        load_weights(1)
-        n2_sb = load_list(n2, "n2_sb")
-        with nc.allow_non_contiguous_dma(reason="one value a row"):
-            nc.sync.dma_start(sl_sb[:], sl.rearrange("(m p) o -> p (m o)", p=P))
-            nc.sync.dma_start(th_sb[:], th.rearrange("(m p) o -> p (m o)", p=P))
-        load_weights(2)
-
-        key_words = reuse.tile([P, H], U32, name="key_words", offset=0)
+        key_words = sb.tile([P, H], U32, name="key_words")
         nc.vector.tensor_copy(key_words[:], d_table[:].indirect(k1_sb[:]))
         key_codes = sb.tile([P, H], U32, name="key_codes", align_bytes=64)
         nc.vector.tensor_copy(
             key_codes[:].bitcast(I32).rearrange("p (t c i) -> p c t i", t=PACK, i=4),
             key_words[:].bitcast(I32).rearrange("p (c i t) -> p c t i", t=PACK, i=4),
         )
+
+        xq_scale = sb.tile([P, S], U8, name="xq_scale", align_bytes=64)
+        x2_scale = sb.tile([P, S], U8, name="x2_scale", align_bytes=64)
+        nc.vector.tensor_copy(xq_scale[:], x_bytes[:].indirect(offs_sb[:]))
 
         xq_codes = sb.tile([P, S], U32, name="xq_codes", align_bytes=64)
         x2_codes = sb.tile([P, S], U32, name="x2_codes", align_bytes=64)
@@ -124,7 +124,7 @@ def tile_picked_kmixierl_none_p_kernel(
         def score(u):
             cols = columns(u)
             nc.vector.tensor_copy(xq_codes[:, cols], x_table[:].indirect(offs_sb[:, entries(u)]))
-            s_ps[u] = psum.tile([P, PACK, HALF], F32, name=f"s_ps{u}")
+            s_ps[u] = psum.tile([P, PACK, HALF], F32, name=f"s_ps{u}", tag=f"s_ps{u}")
             for t in range(PACK):
                 keys = slice(t * P, (t + 1) * P)
                 nc.tensor.matmul_mx(
@@ -161,7 +161,7 @@ def tile_picked_kmixierl_none_p_kernel(
         w_codes, w_scale = {}, {}
 
         def quantize_weights(m):
-            w_bf = sb.tile([P, 2, P, PACK], BF16, name=f"w_bf{m}", tag=f"w_bf{m}", align_bytes=64)
+            w_bf = sb.tile([P, 2, P, PACK], BF16, name=f"w_bf{m}", tag=f"w_bf{max(m - 1, 0)}", align_bytes=64)
             for a, name in enumerate(("w2", "w1")):
                 copy = nc.scalar.copy if m == 0 else nc.vector.tensor_copy
                 copy(
@@ -172,11 +172,6 @@ def tile_picked_kmixierl_none_p_kernel(
             nc.vector.quantize_mx(
                 out=w_codes[m][:].bitcast(FP8X4), scales=w_scale[m][:], in_=w_bf[:].rearrange("p a c j -> p (a c j)")
             )
-
-        minus_sl = sb.tile([P, TILES], F32, name="minus_sl")
-        bias = sb.tile([P, TILES], F32, name="bias")
-        nc.gpsimd.tensor_scalar(minus_sl[:], sl_sb[:], -1.0, 0.0, ALU.mult, ALU.add)
-        nc.gpsimd.tensor_tensor(bias[:], minus_sl[:], th_sb[:], ALU.mult)
 
         h_sb = [sb.tile([P, S], F32, name=f"h_sb{m}") for m in range(TILES)]
         ds = [sb.tile([P, WINDOW], F32, name=f"ds{m}") for m in range(TILES)]
@@ -211,17 +206,27 @@ def tile_picked_kmixierl_none_p_kernel(
             nc.sync.dma_start(out[m * P : (m + 1) * P, cols], res[m][:, cols])
 
         score(0)
-        pick_two(0)
         score(1)
+        nc.vector.tensor_copy(x2_scale[:], x_bytes[:].indirect(two_sb[:]))
         make_z(0)
-        pick_two(1)
+        pick_two(0)
         quantize_z(0)
         quantize_weights(0)
         product(0, columns(0), nc.scalar.copy)
         scatter(0, columns(0))
+        pick_two(1)
         make_z(1)
         quantize_z(1)
         product(0, columns(1), nc.scalar.copy)
+        gate_ps = psum.tile([P, P], F32, name="gate_ps", tag="s_ps1")
+        nc.tensor.transpose(gate_ps[:], gate_rows[:], identity[:])
+        gate = sb.tile([P, 2 * TILES], F32, name="gate")
+        nc.scalar.copy(gate[:], gate_ps[:, 0 : 2 * TILES])
+        sl_sb, th_sb = gate[:, 0:TILES], gate[:, TILES : 2 * TILES]
+        minus_sl = sb.tile([P, TILES], F32, name="minus_sl")
+        bias = sb.tile([P, TILES], F32, name="bias")
+        nc.gpsimd.tensor_scalar(minus_sl[:], sl_sb, -1.0, 0.0, ALU.mult, ALU.add)
+        nc.gpsimd.tensor_tensor(bias[:], minus_sl[:], th_sb, ALU.mult)
         scatter(0, columns(1))
         every = slice(0, S)
         for m in range(1, TILES):

from contextlib import ExitStack

import concourse.mybir as mybir
from concourse.masks import make_identity

K, T, S, N, G, H = 512, 2048, 256, 512, 2048, 512
FLOPS = 2 * S * (K * H + H * N + K * N)

F32 = mybir.dt.float32
BF16 = mybir.dt.bfloat16
I32 = mybir.dt.int32
U32 = mybir.dt.uint32
U16 = mybir.dt.uint16
U8 = mybir.dt.uint8
FP8X4 = mybir.dt.float8_e4m3fn_x4
ALU = mybir.AluOpType
ACT = mybir.ActivationFunctionType

P = 128
PACK = 4
HALF = S // 2
TILES = N // P
WINDOW = 2 * S
W_CHUNKS = ((0, 1), (1, 2), (2, 4))


def tile_picked_kmixierl_none_p_kernel(
    tc, x_words, x_scales, d_words, d_scales, gn, w1, w2, sl, th, offs, k1, two, n1, n2, out
):
    nc = tc.nc
    with ExitStack() as ctx:
        sb = ctx.enter_context(tc.tile_pool(name="sb", bufs=1))
        psum = ctx.enter_context(tc.psum_pool(name="psum", bufs=1))

        def load_list(src, name):
            t = sb.tile(list(src.shape), U16, name=name)
            nc.sync.dma_start(t[:], src)
            return t

        def load_words(src, name):
            t = sb.tile([P, src.shape[2]], U32, name=name)
            nc.sync.dma_start(t[:].bitcast(I32), src[0].rearrange("p n r -> p (n r)").bitcast(I32))
            return t

        d_bytes = sb.tile([P, G], U8, name="d_bytes")
        x_bytes = sb.tile([P, T], U8, name="x_bytes")
        nc.vector.memset(d_bytes[:].bitcast(I32), 0)
        nc.vector.memset(x_bytes[:].bitcast(I32), 0)

        k1_sb = load_list(k1, "k1_sb")
        for q in range(4):
            nc.scalar.dma_start(
                x_bytes[32 * q : 32 * q + 4, :].bitcast(I32), x_scales[0, 4 * q : 4 * q + 4, :].bitcast(I32)
            )
        nc.sync.dma_start(d_bytes[0:P:8, :].bitcast(I32), d_scales[0].bitcast(I32))
        offs_sb = load_list(offs, "offs_sb")
        d_table = load_words(d_words, "d_table")
        two_sb = load_list(two, "two_sb")
        n1_sb = load_list(n1, "n1_sb")
        n2_sb = load_list(n2, "n2_sb")
        x_table = load_words(x_words, "x_table")

        gn_sb = sb.tile([P, PACK], F32, name="gn_sb")
        nc.gpsimd.dma_start(gn_sb[:], gn.rearrange("(p t) o -> p (t o)", t=PACK))
        warm_out = sb.tile([P, 1], F32, name="warm_out")
        nc.scalar.activation(warm_out[:], gn_sb[:, 0:1], ACT.Sigmoid)
        gate_rows = sb.tile([P, P], F32, name="gate_rows")
        identity = sb.tile([P, P], F32, name="identity")
        nc.gpsimd.memset(gate_rows[:], 0.0)
        nc.gpsimd.dma_start(gate_rows[0:TILES, :], sl.rearrange("(m p) o -> m (p o)", p=P))
        nc.gpsimd.dma_start(gate_rows[TILES : 2 * TILES, :], th.rearrange("(m p) o -> m (p o)", p=P))
        make_identity(nc, identity[:])

        raw = {}

        def load_weights(name, w, chunk):
            lo, hi = W_CHUNKS[chunk]
            t = sb.tile([P, PACK, (hi - lo) * P], F32, name=f"{name}_raw{chunk}")
            nc.sync.dma_start(t[:], w[:, lo * P : hi * P].rearrange("(p j) c -> p j c", j=PACK))
            for m in range(lo, hi):
                raw[name, m] = t[:, :, (m - lo) * P : (m - lo + 1) * P]

        for chunk in range(len(W_CHUNKS)):
            load_weights("w2", w2, chunk)
            load_weights("w1", w1, chunk)

        key_bytes = sb.tile([P, H], U8, name="key_bytes")
        nc.vector.tensor_copy(key_bytes[:], d_bytes[:].indirect(k1_sb[:]))
        key_scale = sb.tile([P, H], U8, name="key_scale", align_bytes=64)
        nc.vector.tensor_copy(
            key_scale[:].rearrange("p (t c i) -> p c t i", t=PACK, i=16),
            key_bytes[:].rearrange("p (c i t) -> p c t i", t=PACK, i=16),
        )
        for c in range(1, 4):
            nc.scalar.dma_start(key_scale[c:P:32, :].bitcast(I32), key_scale[8 * c : P : 32, :].bitcast(I32))


        key_words = sb.tile([P, H], U32, name="key_words")
        nc.vector.tensor_copy(key_words[:], d_table[:].indirect(k1_sb[:]))
        key_codes = sb.tile([P, H], U32, name="key_codes", align_bytes=64)
        nc.vector.tensor_copy(
            key_codes[:].bitcast(I32).rearrange("p (t c i) -> p c t i", t=PACK, i=4),
            key_words[:].bitcast(I32).rearrange("p (c i t) -> p c t i", t=PACK, i=4),
        )

        xq_scale = sb.tile([P, S], U8, name="xq_scale", align_bytes=64)
        x2_scale = sb.tile([P, S], U8, name="x2_scale", align_bytes=64)
        nc.vector.tensor_copy(xq_scale[:], x_bytes[:].indirect(offs_sb[:]))

        xq_codes = sb.tile([P, S], U32, name="xq_codes", align_bytes=64)
        x2_codes = sb.tile([P, S], U32, name="x2_codes", align_bytes=64)
        z_bf = {}
        z_codes = sb.tile([P, S], U32, name="z_codes", align_bytes=64)
        z_scale = sb.tile([P, S], U8, name="z_scale", align_bytes=64)

        def columns(u):
            return slice(u * HALF, (u + 1) * HALF)

        def entries(u):
            return slice(u * HALF // 16, (u + 1) * HALF // 16)

        s_ps = {}

        def score(u):
            cols = columns(u)
            nc.vector.tensor_copy(xq_codes[:, cols], x_table[:].indirect(offs_sb[:, entries(u)]))
            s_ps[u] = psum.tile([P, PACK, HALF], F32, name=f"s_ps{u}", tag=f"s_ps{u}")
            for t in range(PACK):
                keys = slice(t * P, (t + 1) * P)
                nc.tensor.matmul_mx(
                    out=s_ps[u][:, t, :],
                    lhsT=key_codes[:, keys].bitcast(FP8X4),
                    lhsT_scale=key_scale[:, keys],
                    rhs=xq_codes[:, cols].bitcast(FP8X4),
                    rhs_scale=xq_scale[:, cols],
                    start=True,
                    stop=True,
                )

        def pick_two(u):
            nc.vector.tensor_copy(x2_codes[:, columns(u)], x_table[:].indirect(two_sb[:, entries(u)]))

        def make_z(u):
            z_bf[u] = sb.tile([P, HALF, PACK], BF16, name=f"z_bf{u}", tag=("z_bf0", "w_bf0")[u], align_bytes=64)
            nc.vector.scalar_tensor_tensor(
                z_bf[u][:],
                s_ps[u][:].rearrange("p t j -> p j t"),
                0.0625,
                gn_sb[:].unsqueeze(1).to_broadcast([P, HALF, PACK]),
                ALU.mult,
                ALU.mult,
            )

        def quantize_z(u):
            nc.vector.quantize_mx(
                out=z_codes[:, columns(u)].bitcast(FP8X4),
                scales=z_scale[:, columns(u)],
                in_=z_bf[u][:].rearrange("p j t -> p (j t)"),
            )

        w_codes, w_scale = {}, {}

        def quantize_weights(m):
            w_bf = sb.tile([P, 2, P, PACK], BF16, name=f"w_bf{m}", tag=f"w_bf{max(m - 1, 0)}", align_bytes=64)
            for a, name in enumerate(("w2", "w1")):
                copy = nc.scalar.copy if m == 0 else nc.vector.tensor_copy
                copy(
                    w_bf[:, a].rearrange("p (c i) j -> p c j i", i=4), raw[name, m].rearrange("p j (c i) -> p c j i", i=4)
                )
            w_codes[m] = sb.tile([P, 2 * P], U32, name=f"w_codes{m}", align_bytes=64)
            w_scale[m] = sb.tile([P, 2 * P], U8, name=f"w_scale{m}", align_bytes=64)
            nc.vector.quantize_mx(
                out=w_codes[m][:].bitcast(FP8X4), scales=w_scale[m][:], in_=w_bf[:].rearrange("p a c j -> p (a c j)")
            )

        h_sb = [sb.tile([P, S], F32, name=f"h_sb{m}") for m in range(TILES)]
        ds = [sb.tile([P, WINDOW], F32, name=f"ds{m}") for m in range(TILES)]
        sg = [sb.tile([P, S], F32, name=f"sg{m}") for m in range(TILES)]
        res = [sb.tile([P, S], F32, name=f"res{m}") for m in range(TILES)]

        def product(m, cols, evacuate):
            h_ps = psum.tile([P, cols.stop - cols.start], F32, name=f"h_ps{m}_{cols.start}")
            for a, (codes, scale) in enumerate(((x2_codes, x2_scale), (z_codes, z_scale))):
                rows = slice(a * P, (a + 1) * P)
                nc.tensor.matmul_mx(
                    out=h_ps[:],
                    lhsT=w_codes[m][:, rows].bitcast(FP8X4),
                    lhsT_scale=w_scale[m][:, rows],
                    rhs=codes[:, cols].bitcast(FP8X4),
                    rhs_scale=scale[:, cols],
                    start=(a == 0),
                    stop=(a == 1),
                )
            evacuate(h_sb[m][:, cols], h_ps[:])

        def scatter(m, cols):
            listed = n1_sb[:, cols.start // 16 : cols.stop // 16]
            nc.scalar.activation(ds[m][:].indirect(listed), h_sb[m][:, cols], ACT.Copy)

        def finish(m, cols, engine):
            listed = n2_sb[:, cols.start // 16 : cols.stop // 16]
            nc.scalar.activation(
                sg[m][:, cols], ds[m][:].indirect(listed), ACT.Sigmoid, bias=bias[:, m : m + 1], scale=sl_sb[:, m : m + 1]
            )
            engine.tensor_tensor(res[m][:, cols], h_sb[m][:, cols], sg[m][:, cols], ALU.mult)
            nc.sync.dma_start(out[m * P : (m + 1) * P, cols], res[m][:, cols])

        score(0)
        score(1)
        nc.vector.tensor_copy(x2_scale[:], x_bytes[:].indirect(two_sb[:]))
        make_z(0)
        pick_two(0)
        quantize_z(0)
        quantize_weights(0)
        product(0, columns(0), nc.scalar.copy)
        scatter(0, columns(0))
        pick_two(1)
        make_z(1)
        quantize_z(1)
        product(0, columns(1), nc.scalar.copy)
        gate_ps = psum.tile([P, P], F32, name="gate_ps", tag="s_ps1")
        nc.tensor.transpose(gate_ps[:], gate_rows[:], identity[:])
        gate = sb.tile([P, 2 * TILES], F32, name="gate")
        nc.scalar.copy(gate[:], gate_ps[:, 0 : 2 * TILES])
        sl_sb, th_sb = gate[:, 0:TILES], gate[:, TILES : 2 * TILES]
        minus_sl = sb.tile([P, TILES], F32, name="minus_sl")
        bias = sb.tile([P, TILES], F32, name="bias")
        nc.gpsimd.tensor_scalar(minus_sl[:], sl_sb, -1.0, 0.0, ALU.mult, ALU.add)
        nc.gpsimd.tensor_tensor(bias[:], minus_sl[:], th_sb, ALU.mult)
        scatter(0, columns(1))
        every = slice(0, S)
        for m in range(1, TILES):
            quantize_weights(m)
            product(m, every, nc.vector.tensor_copy)
            scatter(m, every)
            finish(m - 1, every, nc.gpsimd)
        for u in range(2):
            finish(TILES - 1, columns(u), nc.vector)
